import numpy as np
import ml_dtypes


def mxq(x, axis, fmt="e4m3"):
    dtype, down = {"e4m3": (ml_dtypes.float8_e4m3fn, 7), "e5m2": (ml_dtypes.float8_e5m2, 14)}[fmt]
    v = np.moveaxis(np.asarray(x, np.float32).astype(ml_dtypes.bfloat16).astype(np.float64), axis, -1)
    blocks = v.reshape(v.shape[:-1] + (-1, 32))
    amax = np.abs(blocks).max(-1, keepdims=True)
    byte = np.maximum(np.where(amax > 0, np.frexp(amax)[1] - 1 + 127, 0) - down, 1)
    scale = np.exp2(byte - 127.0)
    codes = (blocks / scale).astype(np.float32).astype(dtype).astype(np.float64)
    return np.moveaxis((codes * scale).reshape(v.shape), -1, axis)


WIDE = False


def mx_kscale(k):
    if not WIDE:
        return np.ones(k)
    levels = np.array([10, -10, 5, -5, 0])
    if k % 512:
        return np.exp2(np.random.permutation(np.resize(levels, k // 32))).repeat(32)
    a = np.empty((k // 512, 16))
    for p in range(k // 512):
        a[p, :8] = np.random.permutation(np.resize(levels, 8))
        for g in range(8):
            far = levels[np.abs(levels - a[p, g]) >= 10]
            a[p, g + 8] = far[np.random.randint(len(far))]
    return np.exp2(a.ravel()).repeat(32)


def f64(x):
    return np.asarray(x).astype(np.float64)


def striped(idx):
    return np.tile(idx.reshape(-1, 16).T, (8, 1)).astype(np.uint16)


def unstriped(offs):
    return offs[:16].T.reshape(-1).astype(np.int64)


def pack_weight(w):
    k, n = w.shape
    w = f64(np.asarray(w, np.float32).astype(ml_dtypes.bfloat16)).reshape(k // 32, 32, n)
    amax = np.abs(w).max(1)
    byte = np.clip(np.where(amax > 0, np.frexp(amax)[1] - 1 + 127 - 7, 1), 1, 254)
    scaled = (w * np.exp2(127.0 - byte)[:, None, :]).reshape(k, n).astype(np.float32)
    words = np.ascontiguousarray(scaled.reshape(k // 512, 128, 4, n).transpose(0, 1, 3, 2)).astype(ml_dtypes.float8_e4m3fn).view(np.uint8)
    return words, np.ascontiguousarray(byte.astype(np.uint8).reshape(k // 512, 16, n))


def unpack_weight(words, scales):
    g, p, n, _ = words.shape
    vals = np.ascontiguousarray(words).view(ml_dtypes.float8_e4m3fn).astype(np.float64) * np.repeat(np.exp2(scales.astype(np.float64) - 127.0), 8, axis=1)[..., None]
    return vals.transpose(0, 1, 3, 2).reshape(g * 512, n)


def relu(v):
    return np.maximum(v, 0.0)


K, T, D, S, V, H, N = 1024, 2048, 4, 512, 256, 1024, 512
P = 2 ** 7


def setup_inputs():
    n = np.random.standard_normal
    s = mx_kscale(K)[:, None]
    u = mx_kscale(H)
    q = np.random.permutation(S)
    packed = pack_weight(n((K, T)) * s)
    return {
        "x_words": packed[0],
        "x_scales": packed[1],
        "w1": (n((K, H)) / np.sqrt(K) / s * u).astype(np.float32),
        "w2": (n((H, N)) / np.sqrt(H) / u[:, None]).astype(np.float32),
        "gate": np.tile(np.random.uniform(0.2, 1.0, (D, 1, V)) / np.sqrt(D), (1, P, 1)).astype(np.float32),
        "offs": striped(np.random.permutation(T)[:S]),
        "pos1": striped(q[:V]),
        "pos2": striped(q[V:]),
        "pos3": striped(np.random.permutation(S)[:V]),
        "pos4": striped(np.random.permutation(S)[:V]),
    }


def reference(x_words, x_scales, w1, w2, gate, offs, pos1, pos2, pos3, pos4):
    h = relu(mxq(f64(w1), 0, "e4m3").T @ unpack_weight(x_words, x_scales)[:, unstriped(offs)])
    z = sum(f64(gate)[d, :1] * h[:, unstriped(p)] for d, p in enumerate((pos1, pos2, pos3, pos4)))
    return mxq(f64(w2), 0, "e4m3").T @ mxq(z, 0, "e4m3")

@@ -1,0 +1,257 @@
+from contextlib import ExitStack
+
+import concourse.mybir as mybir
+from concourse.masks import make_identity
+
+K, T, D, S, V, H, N = 1024, 2048, 4, 512, 256, 1024, 512
+FLOPS = 2 * K * H * S + 2 * H * N * V
+
+F32 = mybir.dt.float32
+BF16 = mybir.dt.bfloat16
+I32 = mybir.dt.int32
+U32 = mybir.dt.uint32
+U16 = mybir.dt.uint16
+U8 = mybir.dt.uint8
+FP8X4 = mybir.dt.float8_e4m3fn_x4
+ACT = mybir.ActivationFunctionType
+MULT = mybir.AluOpType.mult
+
+P = 128
+PACK = 4
+K_PASS = P * PACK
+PASSES = K // K_PASS
+TILES = H // P
+TILES_PER_PASS = K_PASS // P
+HALF = V // 2
+W1_CHUNKS = [(0, 1), (1, 1), (2, 2), (4, 2), (6, 2)]
+
+
+def tile_picked_sage_relu_p_kernel(
+    tc, x_words, x_scales, w1, w2, gate, offs, pos1, pos2, pos3, pos4, out
+):
+    nc = tc.nc
+    with ExitStack() as ctx:
+        keep = ctx.enter_context(tc.tile_pool(name="keep", bufs=1))
+        psum = ctx.enter_context(tc.psum_pool(name="psum", bufs=2))
+
+        def held(name, shape, dtype):
+            return keep.tile(shape, dtype, name=name, align_bytes=64)
+
+        offs_sb = held("offs_sb", [P, S // 16], U16)
+        pos_sb = [held("pos_sb%d" % d, [P, V // 16], U16) for d in range(D)]
+        word_table = [held("word_table%d" % g, [P, T], I32) for g in range(PASSES)]
+        scale_table = held("scale_table", [P, T // 4], I32)
+        gate_sb = held("gate_sb", [P, D, V], F32)
+        ident = held("ident", [P, P], F32)
+        w1_raw = {}
+        for first, count in W1_CHUNKS:
+            for g in range(PASSES):
+                w1_raw[first, g] = held("w1_raw%d_%d" % (first, g), [P, PACK, count * P], F32)
+        w2_raw = [held("w2_raw%d" % g, [P, PACK, N], F32) for g in range(PASSES)]
+
+        nc.vector.memset(scale_table[:], 0)
+        make_identity(nc, ident[:])
+
+        def load_rows(dst, weights, g, cols):
+            rows = weights[g * K_PASS : (g + 1) * K_PASS, cols]
+            nc.sync.dma_start(out=dst[:], in_=rows.rearrange("(p j) c -> p j c", j=PACK))
+
+        def load_w1(chunk):
+            first, count = W1_CHUNKS[chunk]
+            for g in range(PASSES):
+                load_rows(w1_raw[first, g], w1, g, slice(first * P, (first + count) * P))
+
+        def load_gate(d0, d1):
+            nc.sync.dma_start(out=gate_sb[:, d0:d1, :], in_=gate[d0:d1].rearrange("d p v -> p d v"))
+
+        load_w1(0)
+        nc.sync.dma_start(offs_sb[:], offs)
+        for q in range(4):
+            nc.sync.dma_start(
+                out=scale_table[32 * q : 32 * q + 4 * PASSES, :],
+                in_=x_scales[:, 4 * q : 4 * q + 4, :].bitcast(I32),
+            )
+        for g in range(PASSES):
+            nc.sync.dma_start(
+                out=word_table[g][:],
+                in_=x_words[g].rearrange("p c r -> p (c r)").bitcast(I32),
+            )
+        for d, pos in enumerate((pos1, pos2, pos3, pos4)):
+            nc.sync.dma_start(pos_sb[d][:], pos)
+        load_gate(0, 2)
+        load_w1(1)
+        load_gate(2, 4)
+        for chunk in range(2, len(W1_CHUNKS)):
+            load_w1(chunk)
+        for g in range(PASSES):
+            load_rows(w2_raw[g], w2, g, slice(0, N))
+
+        def interleave(dst, raw):
+            nc.scalar.activation(
+                out=dst.rearrange("p (c i) t -> p c t i", i=4),
+                in_=raw.rearrange("p t (c i) -> p c t i", i=4),
+                func=ACT.Copy,
+            )
+
+        def quantize(codes, scales, grouped):
+            nc.vector.quantize_mx(out=codes.bitcast(FP8X4), scales=scales, in_=grouped)
+
+        w1_grouped, w1_codes, w1_scales = {}, {}, {}
+
+        def cast_w1(chunk):
+            first, count = W1_CHUNKS[chunk]
+            w1_grouped[first] = held("w1_grouped%d" % first, [P, PASSES, count * P, PACK], BF16)
+            for g in range(PASSES):
+                interleave(w1_grouped[first][:, g], w1_raw[first, g][:])
+
+        def quantize_w1(chunk):
+            first, count = W1_CHUNKS[chunk]
+            codes = held("w1_codes%d" % first, [P, PASSES, count * P], U32)
+            scales = held("w1_scales%d" % first, [P, PASSES, count * P], U8)
+            quantize(
+                codes[:].rearrange("p g c -> p (g c)"),
+                scales[:].rearrange("p g c -> p (g c)"),
+                w1_grouped[first][:].rearrange("p g c t -> p (g c t)"),
+            )
+            for m in range(count):
+                w1_codes[first + m] = codes[:, :, m * P : (m + 1) * P]
+                w1_scales[first + m] = scales[:, :, m * P : (m + 1) * P]
+
+        cast_w1(0)
+        quantize_w1(0)
+
+        x_codes = [held("x_codes%d" % g, [P, S], U32) for g in range(PASSES)]
+        x_planes = held("x_planes", [P, S], U8)
+        nc.vector.tensor_copy(x_planes[:], scale_table[:].bitcast(U8).indirect(offs_sb[:]))
+        for g in range(PASSES):
+            nc.vector.tensor_copy(x_codes[g][:], word_table[g][:].bitcast(U32).indirect(offs_sb[:]))
+
+        h = {}
+
+        def first_layer(m):
+            acc = psum.tile([P, S], F32, name="h_acc%d" % m, tag="wide")
+            for g in range(PASSES):
+                nc.tensor.matmul_mx(
+                    out=acc[:],
+                    lhsT=w1_codes[m][:, g, :].bitcast(FP8X4),
+                    lhsT_scale=w1_scales[m][:, g, :],
+                    rhs=x_codes[g][:].bitcast(FP8X4),
+                    rhs_scale=x_planes[4 * g :, :],
+                    start=(g == 0),
+                    stop=(g == PASSES - 1),
+                )
+            h[m] = held("h%d" % m, [P, S], F32)
+            nc.scalar.activation(out=h[m][:], in_=acc[:], func=ACT.Relu)
+
+        z_rows = [held("z_rows%d" % g, [P, 2, 2, P, 2], BF16) for g in range(PASSES)]
+
+        def aggregate(m, halves, copy_out):
+            g, mm = divmod(m, TILES_PER_PASS)
+            cols = slice(halves[0] * HALF, (halves[-1] + 1) * HALF)
+            width = len(halves) * HALF
+            terms = []
+            for d in range(D):
+                term = held("term%d_%d_%d" % (m, d, halves[0]), [P, width], F32)
+                offsets = pos_sb[d][:, cols.start // 16 : cols.stop // 16]
+                nc.vector.tensor_tensor(term[:], h[m][:].indirect(offsets), gate_sb[:, d, cols], MULT)
+                terms.append(term)
+            sums = psum.tile([P, len(halves), P], F32, name="sums%d_%d" % (m, halves[0]), tag="sums")
+            for a in range(len(halves)):
+                for d in range(D):
+                    nc.tensor.matmul(
+                        sums[:, a, :],
+                        terms[d][:, a * HALF : (a + 1) * HALF],
+                        ident[:],
+                        start=(d == 0),
+                        stop=(d == D - 1),
+                        is_transpose=True,
+                    )
+            dst = z_rows[g][:, halves[0] : halves[-1] + 1, :, 32 * mm : 32 * (mm + 1), :]
+            copy_out(
+                out=dst.rearrange("v a u q e -> v u a q e"),
+                in_=sums[:].rearrange("v a (q u e) -> v u a q e", u=2, e=2),
+            )
+
+        z_codes = [held("z_codes%d" % g, [P, V], U32) for g in range(PASSES)]
+        z_scales = [held("z_scales%d" % g, [P, V], U8) for g in range(PASSES)]
+
+        def quantize_z(g, halves):
+            cols = slice(halves[0] * HALF, (halves[-1] + 1) * HALF)
+            width = len(halves) * HALF
+            turned = psum.tile([P, 2, width], F32, name="turned%d_%d" % (g, halves[0]), tag="turned")
+            for a, half in enumerate(halves):
+                for u in range(2):
+                    words = z_rows[g][:, half, u].rearrange("v p e -> v (p e)").bitcast(F32)
+                    nc.tensor.transpose(turned[:, u, a * HALF : (a + 1) * HALF], words, ident[:])
+            grouped = held("z_grouped%d_%d" % (g, halves[0]), [P, width * PACK], BF16)
+            nc.scalar.copy(
+                out=grouped[:].bitcast(F32).rearrange("p (v u) -> p v u", u=2),
+                in_=turned[:].rearrange("p u v -> p v u"),
+            )
+            quantize(z_codes[g][:, cols], z_scales[g][:, cols], grouped[:])
+
+        w2_grouped = [held("w2_grouped%d" % g, [P, N, PACK], BF16) for g in range(PASSES)]
+        w2_codes = [held("w2_codes%d" % g, [P, N], U32) for g in range(PASSES)]
+        w2_scales = [held("w2_scales%d" % g, [P, N], U8) for g in range(PASSES)]
+
+        def quantize_w2(g):
+            quantize(w2_codes[g][:], w2_scales[g][:], w2_grouped[g][:].rearrange("p c t -> p (c t)"))
+
+        def second_layer(half, tag, copies):
+            cols = slice(half * HALF, (half + 1) * HALF)
+            for pair, copy_out in enumerate(copies):
+                acc = psum.tile([P, 2, HALF], F32, name="o_acc%d_%d" % (half, pair), tag=tag)
+                for a in range(2):
+                    rows = slice((2 * pair + a) * P, (2 * pair + a + 1) * P)
+                    for g in range(PASSES):
+                        nc.tensor.matmul_mx(
+                            out=acc[:, a, :],
+                            lhsT=w2_codes[g][:, rows].bitcast(FP8X4),
+                            lhsT_scale=w2_scales[g][:, rows],
+                            rhs=z_codes[g][:, cols].bitcast(FP8X4),
+                            rhs_scale=z_scales[g][:, cols],
+                            start=(g == 0),
+                            stop=(g == PASSES - 1),
+                        )
+                result = held("result%d_%d" % (half, pair), [P, 2, HALF], F32)
+                copy_out(out=result[:], in_=acc[:])
+                nc.sync.dma_start(
+                    out=out[2 * pair * P : 2 * (pair + 1) * P, cols].rearrange("(a p) v -> p a v", p=P),
+                    in_=result[:],
+                )
+
+        both = [0, 1]
+        first_layer(0)
+        cast_w1(1)
+        quantize_w1(1)
+        first_layer(1)
+        aggregate(0, both, nc.scalar.copy)
+        cast_w1(2)
+        quantize_w1(2)
+        first_layer(2)
+        aggregate(1, both, nc.scalar.copy)
+        first_layer(3)
+        cast_w1(3)
+        aggregate(2, both, nc.scalar.copy)
+        quantize_w1(3)
+        first_layer(4)
+        aggregate(3, both, nc.scalar.copy)
+        first_layer(5)
+        cast_w1(4)
+        quantize_w1(4)
+        first_layer(6)
+        aggregate(4, both, nc.scalar.copy)
+        first_layer(7)
+        quantize_z(0, both)
+        interleave(w2_grouped[0][:], w2_raw[0][:])
+        aggregate(5, both, nc.scalar.copy)
+        quantize_w2(0)
+        interleave(w2_grouped[1][:], w2_raw[1][:])
+        aggregate(6, both, nc.scalar.copy)
+        quantize_w2(1)
+        aggregate(7, [0], nc.scalar.copy)
+        quantize_z(1, [0])
+        aggregate(7, [1], nc.vector.tensor_copy)
+        second_layer(0, "out", [nc.scalar.copy, nc.scalar.copy])
+        quantize_z(1, [1])
+        second_layer(1, "wide", [nc.vector.tensor_copy, nc.scalar.copy])

@@ -23,7 +23,7 @@ PASSES = K // K_PASS
 TILES = H // P
 TILES_PER_PASS = K_PASS // P
 HALF = V // 2
-W1_CHUNKS = [(0, 1), (1, 1), (2, 2), (4, 2), (6, 2)]
+W1_CHUNKS = [(0, 1), (1, 1), (2, 1), (3, 1), (4, 2), (6, 2)]
 
 
 def tile_picked_sage_relu_p_kernel(
@@ -34,14 +34,15 @@ def tile_picked_sage_relu_p_kernel(
         keep = ctx.enter_context(tc.tile_pool(name="keep", bufs=1))
         psum = ctx.enter_context(tc.psum_pool(name="psum", bufs=2))
 
-        def held(name, shape, dtype):
-            return keep.tile(shape, dtype, name=name, align_bytes=64)
+        def held(name, shape, dtype, slot=None):
+            return keep.tile(shape, dtype, name=name, tag=slot or name, align_bytes=64)
 
         offs_sb = held("offs_sb", [P, S // 16], U16)
         pos_sb = [held("pos_sb%d" % d, [P, V // 16], U16) for d in range(D)]
         word_table = [held("word_table%d" % g, [P, T], I32) for g in range(PASSES)]
         scale_table = held("scale_table", [P, T // 4], I32)
         gate_sb = held("gate_sb", [P, D, V], F32)
+        gate_rows = held("gate_rows", [P, V], F32)
         ident = held("ident", [P, P], F32)
         w1_raw = {}
         for first, count in W1_CHUNKS:
@@ -50,6 +51,7 @@ def tile_picked_sage_relu_p_kernel(
         w2_raw = [held("w2_raw%d" % g, [P, PACK, N], F32) for g in range(PASSES)]
 
         nc.vector.memset(scale_table[:], 0)
+        nc.vector.memset(gate_rows[:], 0.0)
         make_identity(nc, ident[:])
 
         def load_rows(dst, weights, g, cols):
@@ -61,100 +63,130 @@ def tile_picked_sage_relu_p_kernel(
             for g in range(PASSES):
                 load_rows(w1_raw[first, g], w1, g, slice(first * P, (first + count) * P))
 
-        def load_gate(d0, d1):
-            nc.sync.dma_start(out=gate_sb[:, d0:d1, :], in_=gate[d0:d1].rearrange("d p v -> p d v"))
+        def load_scales(g):
+            for q in range(4):
+                nc.sync.dma_start(
+                    out=scale_table[32 * q + 4 * g : 32 * q + 4 * g + 4, :],
+                    in_=x_scales[g, 4 * q : 4 * q + 4, :].bitcast(I32),
+                )
 
-        load_w1(0)
-        nc.sync.dma_start(offs_sb[:], offs)
-        for q in range(4):
-            nc.sync.dma_start(
-                out=scale_table[32 * q : 32 * q + 4 * PASSES, :],
-                in_=x_scales[:, 4 * q : 4 * q + 4, :].bitcast(I32),
-            )
-        for g in range(PASSES):
+        def load_words(g):
             nc.sync.dma_start(
                 out=word_table[g][:],
                 in_=x_words[g].rearrange("p c r -> p (c r)").bitcast(I32),
             )
+
+        nc.sync.dma_start(offs_sb[:], offs)
+        load_w1(0)
+        load_scales(0)
+        load_words(0)
+        nc.sync.dma_start(out=gate_rows[0:D, :], in_=gate[:, 0, :])
+        load_scales(1)
+        load_words(1)
         for d, pos in enumerate((pos1, pos2, pos3, pos4)):
             nc.sync.dma_start(pos_sb[d][:], pos)
-        load_gate(0, 2)
-        load_w1(1)
-        load_gate(2, 4)
-        for chunk in range(2, len(W1_CHUNKS)):
+        for chunk in range(1, len(W1_CHUNKS)):
             load_w1(chunk)
         for g in range(PASSES):
             load_rows(w2_raw[g], w2, g, slice(0, N))
 
+        gate_turned = psum.tile([P, 2, P], F32, name="gate_turned", tag="turned", bufs=1)
+        for a in range(2):
+            nc.tensor.transpose(gate_turned[:, a, :], gate_rows[:, a * HALF : (a + 1) * HALF], ident[:])
+        gate_cols = held("gate_cols", [P, 2, D], F32)
+        nc.scalar.copy(out=gate_cols[:], in_=gate_turned[:, :, 0:D])
+        for pair in range(D // 2):
+            spread = psum.tile([P, 2, V], F32, name="gate_spread%d" % pair, tag="sums")
+            for e in range(2):
+                for a in range(2):
+                    column = gate_cols[:, a, 2 * pair + e : 2 * pair + e + 1]
+                    nc.tensor.transpose(
+                        spread[:, e, a * HALF : (a + 1) * HALF], column.to_broadcast([P, P]), ident[:]
+                    )
+            nc.scalar.copy(out=gate_sb[:, 2 * pair : 2 * pair + 2, :], in_=spread[:])
+
         def interleave(dst, raw):
             nc.scalar.activation(
-                out=dst.rearrange("p (c i) t -> p c t i", i=4),
-                in_=raw.rearrange("p t (c i) -> p c t i", i=4),
+                out=dst.rearrange("p (c i) t -> p c t i", i=2),
+                in_=raw.rearrange("p t (c i) -> p c t i", i=2),
                 func=ACT.Copy,
             )
 
         def quantize(codes, scales, grouped):
             nc.vector.quantize_mx(out=codes.bitcast(FP8X4), scales=scales, in_=grouped)
 
-        w1_grouped, w1_codes, w1_scales = {}, {}, {}
+        w1_codes, w1_scales = {}, {}
 
-        def cast_w1(chunk):
-            first, count = W1_CHUNKS[chunk]
-            w1_grouped[first] = held("w1_grouped%d" % first, [P, PASSES, count * P, PACK], BF16)
+        def quantize_w1(m, by_pass):
+            first = max(f for f, count in W1_CHUNKS if f <= m)
+            cols = slice((m - first) * P, (m - first + 1) * P)
+            grouped = held("w1_grouped%d" % m, [P, PASSES, P, PACK], BF16)
+            w1_codes[m] = held("w1_codes%d" % m, [P, PASSES, P], U32)
+            w1_scales[m] = held("w1_scales%d" % m, [P, PASSES, P], U8)
             for g in range(PASSES):
-                interleave(w1_grouped[first][:, g], w1_raw[first, g][:])
+                interleave(grouped[:, g], w1_raw[first, g][:, :, cols])
+                if by_pass:
+                    quantize(w1_codes[m][:, g], w1_scales[m][:, g], grouped[:, g].rearrange("p c t -> p (c t)"))
+            if not by_pass:
+                quantize(
+                    w1_codes[m][:].rearrange("p g c -> p (g c)"),
+                    w1_scales[m][:].rearrange("p g c -> p (g c)"),
+                    grouped[:].rearrange("p g c t -> p (g c t)"),
+                )
 
-        def quantize_w1(chunk):
-            first, count = W1_CHUNKS[chunk]
-            codes = held("w1_codes%d" % first, [P, PASSES, count * P], U32)
-            scales = held("w1_scales%d" % first, [P, PASSES, count * P], U8)
-            quantize(
-                codes[:].rearrange("p g c -> p (g c)"),
-                scales[:].rearrange("p g c -> p (g c)"),
-                w1_grouped[first][:].rearrange("p g c t -> p (g c t)"),
-            )
-            for m in range(count):
-                w1_codes[first + m] = codes[:, :, m * P : (m + 1) * P]
-                w1_scales[first + m] = scales[:, :, m * P : (m + 1) * P]
-
-        cast_w1(0)
-        quantize_w1(0)
+        quantize_w1(0, False)
 
         x_codes = [held("x_codes%d" % g, [P, S], U32) for g in range(PASSES)]
         x_planes = held("x_planes", [P, S], U8)
         nc.vector.tensor_copy(x_planes[:], scale_table[:].bitcast(U8).indirect(offs_sb[:]))
-        for g in range(PASSES):
-            nc.vector.tensor_copy(x_codes[g][:], word_table[g][:].bitcast(U32).indirect(offs_sb[:]))
+        nc.vector.tensor_copy(x_codes[0][:], word_table[0][:].bitcast(U32).indirect(offs_sb[:]))
+        for a in range(2):
+            nc.vector.tensor_copy(
+                x_codes[1][:, a * V : (a + 1) * V],
+                word_table[1][:].bitcast(U32).indirect(offs_sb[:, a * 16 : (a + 1) * 16]),
+            )
 
         h = {}
 
-        def first_layer(m):
-            acc = psum.tile([P, S], F32, name="h_acc%d" % m, tag="wide")
-            for g in range(PASSES):
-                nc.tensor.matmul_mx(
-                    out=acc[:],
-                    lhsT=w1_codes[m][:, g, :].bitcast(FP8X4),
-                    lhsT_scale=w1_scales[m][:, g, :],
-                    rhs=x_codes[g][:].bitcast(FP8X4),
-                    rhs_scale=x_planes[4 * g :, :],
-                    start=(g == 0),
-                    stop=(g == PASSES - 1),
-                )
+        def relu_scalar(out, in_):
+            nc.scalar.activation(out=out, in_=in_, func=ACT.Relu)
+
+        def relu_vector(out, in_):
+            nc.vector.tensor_scalar_max(out, in_, 0.0)
+
+        def first_layer(m, relus):
             h[m] = held("h%d" % m, [P, S], F32)
-            nc.scalar.activation(out=h[m][:], in_=acc[:], func=ACT.Relu)
+            width = S // len(relus)
+            for a, relu in enumerate(relus):
+                cols = slice(a * width, (a + 1) * width)
+                acc = psum.tile([P, width], F32, name="h_acc%d_%d" % (m, a), tag="wide")
+                for g in range(PASSES):
+                    nc.tensor.matmul_mx(
+                        out=acc[:],
+                        lhsT=w1_codes[m][:, g, :].bitcast(FP8X4),
+                        lhsT_scale=w1_scales[m][:, g, :],
+                        rhs=x_codes[g][:, cols].bitcast(FP8X4),
+                        rhs_scale=x_planes[4 * g :, cols],
+                        start=(g == 0),
+                        stop=(g == PASSES - 1),
+                    )
+                relu(h[m][:, cols], acc[:])
 
         z_rows = [held("z_rows%d" % g, [P, 2, 2, P, 2], BF16) for g in range(PASSES)]
 
-        def aggregate(m, halves, copy_out):
+        def aggregate(m, halves, copy_out, slots=(None, None)):
             g, mm = divmod(m, TILES_PER_PASS)
             cols = slice(halves[0] * HALF, (halves[-1] + 1) * HALF)
             width = len(halves) * HALF
             terms = []
-            for d in range(D):
-                term = held("term%d_%d_%d" % (m, d, halves[0]), [P, width], F32)
-                offsets = pos_sb[d][:, cols.start // 16 : cols.stop // 16]
-                nc.vector.tensor_tensor(term[:], h[m][:].indirect(offsets), gate_sb[:, d, cols], MULT)
-                terms.append(term)
+            for pair in range(D // 2):
+                both_terms = held("terms%d_%d_%d" % (m, halves[0], pair), [P, 2, width], F32, slots[pair])
+                for e in range(2):
+                    d = 2 * pair + e
+                    term = both_terms[:, e, :]
+                    offsets = pos_sb[d][:, cols.start // 16 : cols.stop // 16]
+                    nc.vector.tensor_tensor(term, h[m][:].indirect(offsets), gate_sb[:, d, cols], MULT)
+                    terms.append(term)
             sums = psum.tile([P, len(halves), P], F32, name="sums%d_%d" % (m, halves[0]), tag="sums")
             for a in range(len(halves)):
                 for d in range(D):
@@ -178,7 +210,7 @@ def tile_picked_sage_relu_p_kernel(
         def quantize_z(g, halves):
             cols = slice(halves[0] * HALF, (halves[-1] + 1) * HALF)
             width = len(halves) * HALF
-            turned = psum.tile([P, 2, width], F32, name="turned%d_%d" % (g, halves[0]), tag="turned")
+            turned = psum.tile([P, 2, width], F32, name="turned%d_%d" % (g, halves[0]), tag="turned", bufs=1)
             for a, half in enumerate(halves):
                 for u in range(2):
                     words = z_rows[g][:, half, u].rearrange("v p e -> v (p e)").bitcast(F32)
@@ -197,61 +229,96 @@ def tile_picked_sage_relu_p_kernel(
         def quantize_w2(g):
             quantize(w2_codes[g][:], w2_scales[g][:], w2_grouped[g][:].rearrange("p c t -> p (c t)"))
 
-        def second_layer(half, tag, copies):
+        def second_pass(acc, block, half, g):
+            rows = slice(block * P, (block + 1) * P)
             cols = slice(half * HALF, (half + 1) * HALF)
-            for pair, copy_out in enumerate(copies):
-                acc = psum.tile([P, 2, HALF], F32, name="o_acc%d_%d" % (half, pair), tag=tag)
+            nc.tensor.matmul_mx(
+                out=acc,
+                lhsT=w2_codes[g][:, rows].bitcast(FP8X4),
+                lhsT_scale=w2_scales[g][:, rows],
+                rhs=z_codes[g][:, cols].bitcast(FP8X4),
+                rhs_scale=z_scales[g][:, cols],
+                start=(g == 0),
+                stop=(g == PASSES - 1),
+            )
+
+        def store(result, pair, half):
+            nc.sync.dma_start(
+                out=out[2 * pair * P : 2 * (pair + 1) * P, half * HALF : (half + 1) * HALF].rearrange(
+                    "(a p) v -> p a v", p=P
+                ),
+                in_=result[:],
+            )
+
+        def second_layer_first_half():
+            for pair in range(2):
+                acc = psum.tile([P, 2, HALF], F32, name="o_acc%d" % pair, tag="out", bufs=3)
                 for a in range(2):
-                    rows = slice((2 * pair + a) * P, (2 * pair + a + 1) * P)
                     for g in range(PASSES):
-                        nc.tensor.matmul_mx(
-                            out=acc[:, a, :],
-                            lhsT=w2_codes[g][:, rows].bitcast(FP8X4),
-                            lhsT_scale=w2_scales[g][:, rows],
-                            rhs=z_codes[g][:, cols].bitcast(FP8X4),
-                            rhs_scale=z_scales[g][:, cols],
-                            start=(g == 0),
-                            stop=(g == PASSES - 1),
-                        )
-                result = held("result%d_%d" % (half, pair), [P, 2, HALF], F32)
-                copy_out(out=result[:], in_=acc[:])
-                nc.sync.dma_start(
-                    out=out[2 * pair * P : 2 * (pair + 1) * P, cols].rearrange("(a p) v -> p a v", p=P),
-                    in_=result[:],
-                )
+                        second_pass(acc[:, a, :], 2 * pair + a, 0, g)
+                result = held("result0_%d" % pair, [P, 2, HALF], F32)
+                nc.vector.tensor_copy(out=result[:], in_=acc[:])
+                store(result, pair, 0)
+
+        late = {}
+
+        def open_second_half(block):
+            if block < 2:
+                late[block] = psum.tile([P, HALF], F32, name="late%d" % block, tag="wide")
+            else:
+                late[block] = psum.tile([P, HALF], F32, name="late%d" % block, tag="out", bufs=3)
+            second_pass(late[block][:], block, 1, 0)
+
+        def close_second_half():
+            for pair in range(2):
+                result = held("result1_%d" % pair, [P, 2, HALF], F32)
+                for a, copy_out in enumerate((nc.vector.tensor_copy, nc.scalar.copy)):
+                    block = 2 * pair + a
+                    second_pass(late[block][:], block, 1, 1)
+                    copy_out(out=result[:, a, :], in_=late[block][:])
+                store(result, pair, 1)
+
+        def cast_w2(g, part):
+            cols = slice(part * V, (part + 1) * V)
+            interleave(w2_grouped[g][:, cols], w2_raw[g][:, :, cols])
 
         both = [0, 1]
-        first_layer(0)
-        cast_w1(1)
-        quantize_w1(1)
-        first_layer(1)
-        aggregate(0, both, nc.scalar.copy)
-        cast_w1(2)
-        quantize_w1(2)
-        first_layer(2)
-        aggregate(1, both, nc.scalar.copy)
-        first_layer(3)
-        cast_w1(3)
-        aggregate(2, both, nc.scalar.copy)
-        quantize_w1(3)
-        first_layer(4)
-        aggregate(3, both, nc.scalar.copy)
-        first_layer(5)
-        cast_w1(4)
-        quantize_w1(4)
-        first_layer(6)
-        aggregate(4, both, nc.scalar.copy)
-        first_layer(7)
+        first_layer(0, [relu_scalar, relu_vector])
+        quantize_w1(1, True)
+        first_layer(1, [relu_scalar])
+        quantize_w1(2, False)
+        aggregate(0, both, nc.scalar.copy, (None, "w1_grouped1"))
+        first_layer(2, [relu_scalar])
+        quantize_w1(3, False)
+        first_layer(3, [relu_scalar])
+        aggregate(1, both, nc.scalar.copy, ("w1_grouped2", "w1_grouped3"))
+        quantize_w1(4, False)
+        first_layer(4, [relu_scalar])
+        aggregate(2, both, nc.scalar.copy, (None, "w1_grouped4"))
+        quantize_w1(5, False)
+        first_layer(5, [relu_scalar])
+        aggregate(3, both, nc.scalar.copy, (None, "w1_grouped5"))
+        quantize_w1(6, False)
+        first_layer(6, [relu_scalar])
         quantize_z(0, both)
-        interleave(w2_grouped[0][:], w2_raw[0][:])
-        aggregate(5, both, nc.scalar.copy)
+        aggregate(4, both, nc.scalar.copy, (None, "w1_grouped6"))
+        quantize_w1(7, False)
+        first_layer(7, [relu_scalar])
+        cast_w2(0, 0)
+        cast_w2(0, 1)
         quantize_w2(0)
-        interleave(w2_grouped[1][:], w2_raw[1][:])
-        aggregate(6, both, nc.scalar.copy)
+        aggregate(5, both, nc.scalar.copy, ("z_grouped0_0", "w1_grouped7"))
+        cast_w2(1, 0)
+        cast_w2(1, 1)
         quantize_w2(1)
-        aggregate(7, [0], nc.scalar.copy)
+        aggregate(6, [0], nc.scalar.copy)
+        aggregate(7, [0], nc.scalar.copy, ("w2_grouped0", None))
+        for block in range(3):
+            open_second_half(block)
         quantize_z(1, [0])
-        aggregate(7, [1], nc.vector.tensor_copy)
-        second_layer(0, "out", [nc.scalar.copy, nc.scalar.copy])
+        aggregate(6, [1], nc.scalar.copy)
+        aggregate(7, [1], nc.vector.tensor_copy, ("w2_grouped1", "z_grouped1_0"))
         quantize_z(1, [1])
-        second_layer(1, "wide", [nc.vector.tensor_copy, nc.scalar.copy])
+        second_layer_first_half()
+        open_second_half(3)
+        close_second_half()

@@ -63,11 +63,11 @@ def tile_picked_sage_relu_p_kernel(
             for g in range(PASSES):
                 load_rows(w1_raw[first, g], w1, g, slice(first * P, (first + count) * P))
 
-        def load_scales(g):
+        def load_scales():
             for q in range(4):
                 nc.sync.dma_start(
-                    out=scale_table[32 * q + 4 * g : 32 * q + 4 * g + 4, :],
-                    in_=x_scales[g, 4 * q : 4 * q + 4, :].bitcast(I32),
+                    out=scale_table[32 * q : 32 * q + 4 * PASSES, :],
+                    in_=x_scales[:, 4 * q : 4 * q + 4, :].bitcast(I32),
                 )
 
         def load_words(g):
@@ -78,10 +78,9 @@ def tile_picked_sage_relu_p_kernel(
 
         nc.sync.dma_start(offs_sb[:], offs)
         load_w1(0)
-        load_scales(0)
-        load_words(0)
         nc.sync.dma_start(out=gate_rows[0:D, :], in_=gate[:, 0, :])
-        load_scales(1)
+        load_words(0)
+        load_scales()
         load_words(1)
         for d, pos in enumerate((pos1, pos2, pos3, pos4)):
             nc.sync.dma_start(pos_sb[d][:], pos)
@@ -117,22 +116,24 @@ def tile_picked_sage_relu_p_kernel(
 
         w1_codes, w1_scales = {}, {}
 
-        def quantize_w1(m, by_pass):
-            first = max(f for f, count in W1_CHUNKS if f <= m)
-            cols = slice((m - first) * P, (m - first + 1) * P)
-            grouped = held("w1_grouped%d" % m, [P, PASSES, P, PACK], BF16)
-            w1_codes[m] = held("w1_codes%d" % m, [P, PASSES, P], U32)
-            w1_scales[m] = held("w1_scales%d" % m, [P, PASSES, P], U8)
+        def quantize_w1(chunk, by_pass):
+            first, count = W1_CHUNKS[chunk]
+            grouped = held("w1_grouped%d" % first, [P, PASSES, count * P, PACK], BF16)
+            codes = held("w1_codes%d" % first, [P, PASSES, count * P], U32)
+            scales = held("w1_scales%d" % first, [P, PASSES, count * P], U8)
             for g in range(PASSES):
-                interleave(grouped[:, g], w1_raw[first, g][:, :, cols])
+                interleave(grouped[:, g], w1_raw[first, g][:])
                 if by_pass:
-                    quantize(w1_codes[m][:, g], w1_scales[m][:, g], grouped[:, g].rearrange("p c t -> p (c t)"))
+                    quantize(codes[:, g], scales[:, g], grouped[:, g].rearrange("p c t -> p (c t)"))
             if not by_pass:
                 quantize(
-                    w1_codes[m][:].rearrange("p g c -> p (g c)"),
-                    w1_scales[m][:].rearrange("p g c -> p (g c)"),
+                    codes[:].rearrange("p g c -> p (g c)"),
+                    scales[:].rearrange("p g c -> p (g c)"),
                     grouped[:].rearrange("p g c t -> p (g c t)"),
                 )
+            for m in range(count):
+                w1_codes[first + m] = codes[:, :, m * P : (m + 1) * P]
+                w1_scales[first + m] = scales[:, :, m * P : (m + 1) * P]
 
         quantize_w1(0, False)
 
@@ -283,41 +284,38 @@ def tile_picked_sage_relu_p_kernel(
             interleave(w2_grouped[g][:, cols], w2_raw[g][:, :, cols])
 
         both = [0, 1]
-        first_layer(0, [relu_scalar, relu_vector])
+        first_layer(0, [relu_scalar, relu_scalar])
         quantize_w1(1, True)
         first_layer(1, [relu_scalar])
         quantize_w1(2, False)
-        aggregate(0, both, nc.scalar.copy, (None, "w1_grouped1"))
+        aggregate(0, both, nc.scalar.copy, (None, "w1_raw1_1"))
         first_layer(2, [relu_scalar])
         quantize_w1(3, False)
         first_layer(3, [relu_scalar])
-        aggregate(1, both, nc.scalar.copy, ("w1_grouped2", "w1_grouped3"))
+        aggregate(1, both, nc.scalar.copy, ("w1_raw2_1", "w1_raw3_1"))
         quantize_w1(4, False)
         first_layer(4, [relu_scalar])
-        aggregate(2, both, nc.scalar.copy, (None, "w1_grouped4"))
-        quantize_w1(5, False)
+        aggregate(2, both, nc.scalar.copy)
         first_layer(5, [relu_scalar])
-        aggregate(3, both, nc.scalar.copy, (None, "w1_grouped5"))
-        quantize_w1(6, False)
+        aggregate(3, both, nc.scalar.copy, ("w1_raw4_1", None))
+        quantize_w1(5, False)
         first_layer(6, [relu_scalar])
         quantize_z(0, both)
-        aggregate(4, both, nc.scalar.copy, (None, "w1_grouped6"))
-        quantize_w1(7, False)
+        aggregate(4, both, nc.scalar.copy)
         first_layer(7, [relu_scalar])
         cast_w2(0, 0)
         cast_w2(0, 1)
         quantize_w2(0)
-        aggregate(5, both, nc.scalar.copy, ("z_grouped0_0", "w1_grouped7"))
+        aggregate(5, both, nc.scalar.copy, ("w1_raw6_1", None))
         cast_w2(1, 0)
         cast_w2(1, 1)
-        quantize_w2(1)
-        aggregate(6, [0], nc.scalar.copy)
-        aggregate(7, [0], nc.scalar.copy, ("w2_grouped0", None))
+        aggregate(6, both, nc.scalar.copy, ("w2_raw0", None))
         for block in range(3):
             open_second_half(block)
+        aggregate(7, [0], nc.scalar.copy)
+        aggregate(7, [1], nc.vector.tensor_copy)
+        quantize_w2(1)
         quantize_z(1, [0])
-        aggregate(6, [1], nc.scalar.copy)
-        aggregate(7, [1], nc.vector.tensor_copy, ("w2_grouped1", "z_grouped1_0"))
         quantize_z(1, [1])
         second_layer_first_half()
         open_second_half(3)

from contextlib import ExitStack

import concourse.mybir as mybir
from concourse.masks import make_identity

K, T, D, S, V, H, N = 1024, 2048, 4, 512, 256, 1024, 512
FLOPS = 2 * K * H * S + 2 * H * N * V

F32 = mybir.dt.float32
BF16 = mybir.dt.bfloat16
I32 = mybir.dt.int32
U32 = mybir.dt.uint32
U16 = mybir.dt.uint16
U8 = mybir.dt.uint8
FP8X4 = mybir.dt.float8_e4m3fn_x4
ACT = mybir.ActivationFunctionType
MULT = mybir.AluOpType.mult

P = 128
PACK = 4
K_PASS = P * PACK
PASSES = K // K_PASS
TILES = H // P
TILES_PER_PASS = K_PASS // P
HALF = V // 2
W1_CHUNKS = [(0, 1), (1, 1), (2, 1), (3, 1), (4, 2), (6, 2)]


def tile_picked_sage_relu_p_kernel(
    tc, x_words, x_scales, w1, w2, gate, offs, pos1, pos2, pos3, pos4, out
):
    nc = tc.nc
    with ExitStack() as ctx:
        keep = ctx.enter_context(tc.tile_pool(name="keep", bufs=1))
        psum = ctx.enter_context(tc.psum_pool(name="psum", bufs=2))

        def held(name, shape, dtype, slot=None):
            return keep.tile(shape, dtype, name=name, tag=slot or name, align_bytes=64)

        offs_sb = held("offs_sb", [P, S // 16], U16)
        pos_sb = [held("pos_sb%d" % d, [P, V // 16], U16) for d in range(D)]
        word_table = [held("word_table%d" % g, [P, T], I32) for g in range(PASSES)]
        scale_table = held("scale_table", [P, T // 4], I32)
        gate_sb = held("gate_sb", [P, D, V], F32)
        gate_rows = held("gate_rows", [P, V], F32)
        ident = held("ident", [P, P], F32)
        w1_raw = {}
        for first, count in W1_CHUNKS:
            for g in range(PASSES):
                w1_raw[first, g] = held("w1_raw%d_%d" % (first, g), [P, PACK, count * P], F32)
        w2_raw = [held("w2_raw%d" % g, [P, PACK, N], F32) for g in range(PASSES)]

        nc.vector.memset(scale_table[:], 0)
        nc.vector.memset(gate_rows[:], 0.0)
        make_identity(nc, ident[:])

        def load_rows(dst, weights, g, cols):
            rows = weights[g * K_PASS : (g + 1) * K_PASS, cols]
            nc.sync.dma_start(out=dst[:], in_=rows.rearrange("(p j) c -> p j c", j=PACK))

        def load_w1(chunk):
            first, count = W1_CHUNKS[chunk]
            for g in range(PASSES):
                load_rows(w1_raw[first, g], w1, g, slice(first * P, (first + count) * P))

        def load_scales():
            for q in range(4):
                nc.sync.dma_start(
                    out=scale_table[32 * q : 32 * q + 4 * PASSES, :],
                    in_=x_scales[:, 4 * q : 4 * q + 4, :].bitcast(I32),
                )

        def load_words(g):
            nc.sync.dma_start(
                out=word_table[g][:],
                in_=x_words[g].rearrange("p c r -> p (c r)").bitcast(I32),
            )

        nc.sync.dma_start(offs_sb[:], offs)
        load_w1(0)
        nc.sync.dma_start(out=gate_rows[0:D, :], in_=gate[:, 0, :])
        load_words(0)
        load_scales()
        load_words(1)
        for d, pos in enumerate((pos1, pos2, pos3, pos4)):
            nc.sync.dma_start(pos_sb[d][:], pos)
        for chunk in range(1, len(W1_CHUNKS)):
            load_w1(chunk)
        for g in range(PASSES):
            load_rows(w2_raw[g], w2, g, slice(0, N))

        gate_turned = psum.tile([P, 2, P], F32, name="gate_turned", tag="turned", bufs=1)
        for a in range(2):
            nc.tensor.transpose(gate_turned[:, a, :], gate_rows[:, a * HALF : (a + 1) * HALF], ident[:])
        gate_cols = held("gate_cols", [P, 2, D], F32)
        nc.scalar.copy(out=gate_cols[:], in_=gate_turned[:, :, 0:D])
        for pair in range(D // 2):
            spread = psum.tile([P, 2, V], F32, name="gate_spread%d" % pair, tag="sums")
            for e in range(2):
                for a in range(2):
                    column = gate_cols[:, a, 2 * pair + e : 2 * pair + e + 1]
                    nc.tensor.transpose(
                        spread[:, e, a * HALF : (a + 1) * HALF], column.to_broadcast([P, P]), ident[:]
                    )
            nc.scalar.copy(out=gate_sb[:, 2 * pair : 2 * pair + 2, :], in_=spread[:])

        def interleave(dst, raw):
            nc.scalar.activation(
                out=dst.rearrange("p (c i) t -> p c t i", i=2),
                in_=raw.rearrange("p t (c i) -> p c t i", i=2),
                func=ACT.Copy,
            )

        def quantize(codes, scales, grouped):
            nc.vector.quantize_mx(out=codes.bitcast(FP8X4), scales=scales, in_=grouped)

        w1_codes, w1_scales = {}, {}

        def quantize_w1(chunk, by_pass):
            first, count = W1_CHUNKS[chunk]
            grouped = held("w1_grouped%d" % first, [P, PASSES, count * P, PACK], BF16)
            codes = held("w1_codes%d" % first, [P, PASSES, count * P], U32)
            scales = held("w1_scales%d" % first, [P, PASSES, count * P], U8)
            for g in range(PASSES):
                interleave(grouped[:, g], w1_raw[first, g][:])
                if by_pass:
                    quantize(codes[:, g], scales[:, g], grouped[:, g].rearrange("p c t -> p (c t)"))
            if not by_pass:
                quantize(
                    codes[:].rearrange("p g c -> p (g c)"),
                    scales[:].rearrange("p g c -> p (g c)"),
                    grouped[:].rearrange("p g c t -> p (g c t)"),
                )
            for m in range(count):
                w1_codes[first + m] = codes[:, :, m * P : (m + 1) * P]
                w1_scales[first + m] = scales[:, :, m * P : (m + 1) * P]

        quantize_w1(0, False)

        x_codes = [held("x_codes%d" % g, [P, S], U32) for g in range(PASSES)]
        x_planes = held("x_planes", [P, S], U8)
        nc.vector.tensor_copy(x_planes[:], scale_table[:].bitcast(U8).indirect(offs_sb[:]))
        nc.vector.tensor_copy(x_codes[0][:], word_table[0][:].bitcast(U32).indirect(offs_sb[:]))
        for a in range(2):
            nc.vector.tensor_copy(
                x_codes[1][:, a * V : (a + 1) * V],
                word_table[1][:].bitcast(U32).indirect(offs_sb[:, a * 16 : (a + 1) * 16]),
            )

        h = {}

        def relu_scalar(out, in_):
            nc.scalar.activation(out=out, in_=in_, func=ACT.Relu)

        def relu_vector(out, in_):
            nc.vector.tensor_scalar_max(out, in_, 0.0)

        def first_layer(m, relus):
            h[m] = held("h%d" % m, [P, S], F32)
            width = S // len(relus)
            for a, relu in enumerate(relus):
                cols = slice(a * width, (a + 1) * width)
                acc = psum.tile([P, width], F32, name="h_acc%d_%d" % (m, a), tag="wide")
                for g in range(PASSES):
                    nc.tensor.matmul_mx(
                        out=acc[:],
                        lhsT=w1_codes[m][:, g, :].bitcast(FP8X4),
                        lhsT_scale=w1_scales[m][:, g, :],
                        rhs=x_codes[g][:, cols].bitcast(FP8X4),
                        rhs_scale=x_planes[4 * g :, cols],
                        start=(g == 0),
                        stop=(g == PASSES - 1),
                    )
                relu(h[m][:, cols], acc[:])

        z_rows = [held("z_rows%d" % g, [P, 2, 2, P, 2], BF16) for g in range(PASSES)]

        def aggregate(m, halves, copy_out, slots=(None, None)):
            g, mm = divmod(m, TILES_PER_PASS)
            cols = slice(halves[0] * HALF, (halves[-1] + 1) * HALF)
            width = len(halves) * HALF
            terms = []
            for pair in range(D // 2):
                both_terms = held("terms%d_%d_%d" % (m, halves[0], pair), [P, 2, width], F32, slots[pair])
                for e in range(2):
                    d = 2 * pair + e
                    term = both_terms[:, e, :]
                    offsets = pos_sb[d][:, cols.start // 16 : cols.stop // 16]
                    nc.vector.tensor_tensor(term, h[m][:].indirect(offsets), gate_sb[:, d, cols], MULT)
                    terms.append(term)
            sums = psum.tile([P, len(halves), P], F32, name="sums%d_%d" % (m, halves[0]), tag="sums")
            for a in range(len(halves)):
                for d in range(D):
                    nc.tensor.matmul(
                        sums[:, a, :],
                        terms[d][:, a * HALF : (a + 1) * HALF],
                        ident[:],
                        start=(d == 0),
                        stop=(d == D - 1),
                        is_transpose=True,
                    )
            dst = z_rows[g][:, halves[0] : halves[-1] + 1, :, 32 * mm : 32 * (mm + 1), :]
            copy_out(
                out=dst.rearrange("v a u q e -> v u a q e"),
                in_=sums[:].rearrange("v a (q u e) -> v u a q e", u=2, e=2),
            )

        z_codes = [held("z_codes%d" % g, [P, V], U32) for g in range(PASSES)]
        z_scales = [held("z_scales%d" % g, [P, V], U8) for g in range(PASSES)]

        def quantize_z(g, halves):
            cols = slice(halves[0] * HALF, (halves[-1] + 1) * HALF)
            width = len(halves) * HALF
            turned = psum.tile([P, 2, width], F32, name="turned%d_%d" % (g, halves[0]), tag="turned", bufs=1)
            for a, half in enumerate(halves):
                for u in range(2):
                    words = z_rows[g][:, half, u].rearrange("v p e -> v (p e)").bitcast(F32)
                    nc.tensor.transpose(turned[:, u, a * HALF : (a + 1) * HALF], words, ident[:])
            grouped = held("z_grouped%d_%d" % (g, halves[0]), [P, width * PACK], BF16)
            nc.scalar.copy(
                out=grouped[:].bitcast(F32).rearrange("p (v u) -> p v u", u=2),
                in_=turned[:].rearrange("p u v -> p v u"),
            )
            quantize(z_codes[g][:, cols], z_scales[g][:, cols], grouped[:])

        w2_grouped = [held("w2_grouped%d" % g, [P, N, PACK], BF16) for g in range(PASSES)]
        w2_codes = [held("w2_codes%d" % g, [P, N], U32) for g in range(PASSES)]
        w2_scales = [held("w2_scales%d" % g, [P, N], U8) for g in range(PASSES)]

        def quantize_w2(g):
            quantize(w2_codes[g][:], w2_scales[g][:], w2_grouped[g][:].rearrange("p c t -> p (c t)"))

        def second_pass(acc, block, half, g):
            rows = slice(block * P, (block + 1) * P)
            cols = slice(half * HALF, (half + 1) * HALF)
            nc.tensor.matmul_mx(
                out=acc,
                lhsT=w2_codes[g][:, rows].bitcast(FP8X4),
                lhsT_scale=w2_scales[g][:, rows],
                rhs=z_codes[g][:, cols].bitcast(FP8X4),
                rhs_scale=z_scales[g][:, cols],
                start=(g == 0),
                stop=(g == PASSES - 1),
            )

        def store(result, pair, half):
            nc.sync.dma_start(
                out=out[2 * pair * P : 2 * (pair + 1) * P, half * HALF : (half + 1) * HALF].rearrange(
                    "(a p) v -> p a v", p=P
                ),
                in_=result[:],
            )

        def second_layer_first_half():
            for pair in range(2):
                acc = psum.tile([P, 2, HALF], F32, name="o_acc%d" % pair, tag="out", bufs=3)
                for a in range(2):
                    for g in range(PASSES):
                        second_pass(acc[:, a, :], 2 * pair + a, 0, g)
                result = held("result0_%d" % pair, [P, 2, HALF], F32)
                nc.vector.tensor_copy(out=result[:], in_=acc[:])
                store(result, pair, 0)

        late = {}

        def open_second_half(block):
            if block < 2:
                late[block] = psum.tile([P, HALF], F32, name="late%d" % block, tag="wide")
            else:
                late[block] = psum.tile([P, HALF], F32, name="late%d" % block, tag="out", bufs=3)
            second_pass(late[block][:], block, 1, 0)

        def close_second_half():
            for pair in range(2):
                result = held("result1_%d" % pair, [P, 2, HALF], F32)
                for a, copy_out in enumerate((nc.vector.tensor_copy, nc.scalar.copy)):
                    block = 2 * pair + a
                    second_pass(late[block][:], block, 1, 1)
                    copy_out(out=result[:, a, :], in_=late[block][:])
                store(result, pair, 1)

        def cast_w2(g, part):
            cols = slice(part * V, (part + 1) * V)
            interleave(w2_grouped[g][:, cols], w2_raw[g][:, :, cols])

        both = [0, 1]
        first_layer(0, [relu_scalar, relu_scalar])
        quantize_w1(1, True)
        first_layer(1, [relu_scalar])
        quantize_w1(2, False)
        aggregate(0, both, nc.scalar.copy, (None, "w1_raw1_1"))
        first_layer(2, [relu_scalar])
        quantize_w1(3, False)
        first_layer(3, [relu_scalar])
        aggregate(1, both, nc.scalar.copy, ("w1_raw2_1", "w1_raw3_1"))
        quantize_w1(4, False)
        first_layer(4, [relu_scalar])
        aggregate(2, both, nc.scalar.copy)
        first_layer(5, [relu_scalar])
        aggregate(3, both, nc.scalar.copy, ("w1_raw4_1", None))
        quantize_w1(5, False)
        first_layer(6, [relu_scalar])
        quantize_z(0, both)
        aggregate(4, both, nc.scalar.copy)
        first_layer(7, [relu_scalar])
        cast_w2(0, 0)
        cast_w2(0, 1)
        quantize_w2(0)
        aggregate(5, both, nc.scalar.copy, ("w1_raw6_1", None))
        cast_w2(1, 0)
        cast_w2(1, 1)
        aggregate(6, both, nc.scalar.copy, ("w2_raw0", None))
        for block in range(3):
            open_second_half(block)
        aggregate(7, [0], nc.scalar.copy)
        aggregate(7, [1], nc.vector.tensor_copy)
        quantize_w2(1)
        quantize_z(1, [0])
        quantize_z(1, [1])
        second_layer_first_half()
        open_second_half(3)
        close_second_half()
